import numpy as np
import ml_dtypes


def mxq(x, axis, fmt="e4m3"):
    dtype, down = {"e4m3": (ml_dtypes.float8_e4m3fn, 7), "e5m2": (ml_dtypes.float8_e5m2, 14)}[fmt]
    v = np.moveaxis(np.asarray(x, np.float32).astype(ml_dtypes.bfloat16).astype(np.float64), axis, -1)
    blocks = v.reshape(v.shape[:-1] + (-1, 32))
    amax = np.abs(blocks).max(-1, keepdims=True)
    byte = np.maximum(np.where(amax > 0, np.frexp(amax)[1] - 1 + 127, 0) - down, 1)
    scale = np.exp2(byte - 127.0)
    codes = (blocks / scale).astype(np.float32).astype(dtype).astype(np.float64)
    return np.moveaxis((codes * scale).reshape(v.shape), -1, axis)


WIDE = False


def mx_kscale(k):
    if not WIDE:
        return np.ones(k)
    levels = np.array([10, -10, 5, -5, 0])
    if k % 512:
        return np.exp2(np.random.permutation(np.resize(levels, k // 32))).repeat(32)
    a = np.empty((k // 512, 16))
    for p in range(k // 512):
        a[p, :8] = np.random.permutation(np.resize(levels, 8))
        for g in range(8):
            far = levels[np.abs(levels - a[p, g]) >= 10]
            a[p, g + 8] = far[np.random.randint(len(far))]
    return np.exp2(a.ravel()).repeat(32)


BF16 = ml_dtypes.bfloat16


def bf(x):
    return np.asarray(x, np.float32).astype(BF16)


def f64(x):
    return np.asarray(x).astype(np.float64)


E2M1 = np.array([0.0, 0.5, 1.0, 1.5, 2.0, 3.0, 4.0, 6.0, -0.0, -0.5, -1.0, -1.5, -2.0, -3.0, -4.0, -6.0])


def pack_weight(w, fmt):
    k, n = w.shape
    w = f64(bf(w)).reshape(k // 32, 32, n)
    amax = np.abs(w).max(1)
    if fmt == "e4m3":
        byte = np.frexp(amax)[1] - 1 + 127 - 7
    else:
        mant, ex = np.frexp(amax / 6.0)
        byte = np.where(mant > 0.5, ex, ex - 1) + 127
    byte = np.clip(np.where(amax > 0, byte, 1), 1, 254)
    scaled = (w * np.exp2(127.0 - byte)[:, None, :]).reshape(k, n).astype(np.float32)
    by_word = np.ascontiguousarray(scaled.reshape(k // 512, 128, 4, n).transpose(0, 1, 3, 2))
    if fmt == "e4m3":
        words = by_word.astype(ml_dtypes.float8_e4m3fn).view(np.uint8)
    else:
        c = by_word.astype(ml_dtypes.float4_e2m1fn).view(np.uint8) & 0xF
        words = c[..., 0::2] | (c[..., 1::2] << 4)
    return np.ascontiguousarray(words), np.ascontiguousarray(byte.astype(np.uint8).reshape(k // 512, 16, n))


def unpack_weight(words, scales, fmt):
    g, p, n, _ = words.shape
    if fmt == "e4m3":
        vals = np.ascontiguousarray(words).view(ml_dtypes.float8_e4m3fn).astype(np.float64)
    else:
        nib = np.empty((g, p, n, 4), np.uint8)
        nib[..., 0::2] = words & 0xF
        nib[..., 1::2] = words >> 4
        vals = E2M1[nib]
    vals = vals * np.repeat(np.exp2(scales.astype(np.float64) - 127.0), 8, axis=1)[..., None]
    return vals.transpose(0, 1, 3, 2).reshape(g * 512, n)
def pack4(w):
    words, scales = pack_weight(w, "e2m1")
    return words.reshape(words.shape[0], 128, -1), scales


def unpack4(words, scales):
    return unpack_weight(words.reshape(words.shape[0], 128, -1, 2), scales, "e2m1")


M, N = 1024, 1536

BETA = 0.9


def setup_inputs():
    s, t = mx_kscale(M), mx_kscale(N)
    left = np.random.standard_normal((M, M)) / np.sqrt(M) * s[:, None]
    grad = np.random.standard_normal((M, N)) / s[:, None] * t
    right = np.random.standard_normal((N, N)) / np.sqrt(N) / t[:, None]
    a_words, a_scales = pack4(left)
    g_words, g_scales = pack4(grad)
    r_words, r_scales = pack_weight(right, "e4m3")
    return {"a_words": a_words, "a_scales": a_scales,
            "g_words": g_words, "g_scales": g_scales,
            "r_words": r_words, "r_scales": r_scales,
            "mom": bf(np.random.standard_normal((M, N)) * t),
            "step": bf(0.5 * np.exp(0.3 * np.random.standard_normal(M))),
            "w": bf(0.5 * np.random.standard_normal((M, N)))}


def reference(a_words, a_scales, g_words, g_scales, r_words, r_scales, mom, step, w):
    a = unpack4(a_words, a_scales)
    g = unpack4(g_words, g_scales)
    r = unpack_weight(r_words, r_scales, "e4m3")
    h = (a.T @ g) + BETA * f64(mom)
    u = mxq(h, 1, "e4m3") @ r
    return f64(w) - f64(step)[:, None] * u

from contextlib import ExitStack

import concourse.mybir as mybir
from concourse.masks import make_identity

M, N = 1024, 1536
BETA = 0.9
FLOPS = 2 * M * M * N + 2 * M * N * N

F32 = mybir.dt.float32
BF16 = mybir.dt.bfloat16
I32 = mybir.dt.int32
U32 = mybir.dt.uint32
U8 = mybir.dt.uint8
FP4X4 = mybir.dt.float4_e2m1fn_x4
FP8X4 = mybir.dt.float8_e4m3fn_x4
MULT = mybir.AluOpType.mult
ADD = mybir.AluOpType.add

P = 128
BANK = 512
ROW_TILES = M // P
LEFT_PASSES = M // BANK
GROUPS = N // BANK
A_FIRST = 2


def tile_two_sided_preconditioner_step_s4_kernel(
    tc, a_words, a_scales, g_words, g_scales, r_words, r_scales, mom, step, w, out
):
    nc = tc.nc
    with ExitStack() as ctx:
        keep = ctx.enter_context(tc.tile_pool(name="keep", bufs=1))
        stage = ctx.enter_context(tc.tile_pool(name="stage", bufs=1))
        psum = ctx.enter_context(tc.psum_pool(name="psum", bufs=8))
        ctx.enter_context(tc.manual_schedule())

        def resident(name, shape, dtype):
            return keep.tile(shape, dtype, name=name, align_bytes=64)

        g_plane = resident("g_plane", [P, LEFT_PASSES, N], U8)
        a_plane = resident("a_plane", [P, LEFT_PASSES, M], U8)
        r_plane = resident("r_plane", [P, N], U8)
        nc.vector.memset(g_plane[:].bitcast(I32), 0)
        nc.vector.memset(a_plane[:].bitcast(I32), 0)
        nc.vector.memset(r_plane[:].bitcast(I32), 0)

        ident = resident("ident", [P, P], F32)
        make_identity(nc, ident[:])
        step_rows = resident("step_rows", [P, P], F32)
        nc.gpsimd.memset(step_rows[:], 0.0)

        def load_words(name, words, first, count):
            t = resident(name, [P, LEFT_PASSES, count], U8)
            src = words.rearrange("g p b -> p g b")[:, :, first : first + count]
            nc.sync.dma_start(out=t[:].bitcast(I32), in_=src.bitcast(I32))
            return t

        def load_plane(plane, scales):
            for r in range(4):
                src = scales[:, r:16:4, :].rearrange("g q n -> q g n")
                nc.sync.dma_start(out=plane[r:P:32, :, :].bitcast(I32), in_=src.bitcast(I32))

        def load_rows(name, matrix, i):
            t = resident("%s%d" % (name, i), [P, N], BF16)
            nc.sync.dma_start(out=t[:], in_=matrix[i * P : (i + 1) * P, :])
            return t

        g_first = load_words("g_first", g_words, 0, 2 * BANK)
        a_first = load_words("a_first", a_words, 0, 2 * P * A_FIRST)
        load_plane(g_plane, g_scales)
        load_plane(a_plane, a_scales)
        g_rest = load_words("g_rest", g_words, 2 * BANK, 2 * (N - BANK))
        mom_t = [load_rows("mom", mom, 0)]
        a_rest = load_words("a_rest", a_words, 2 * P * A_FIRST, 2 * (M - P * A_FIRST))
        for i in range(1, 3):
            mom_t.append(load_rows("mom", mom, i))
        step_raw = resident("step_raw", [ROW_TILES, P], BF16)
        nc.sync.dma_start(out=step_raw[:], in_=step.rearrange("(t p) -> t p", p=P))
        for q in range(4):
            nc.gpsimd.dma_start(
                out=r_plane[32 * q : 32 * q + 4 * GROUPS, :].bitcast(I32),
                in_=r_scales[:, 4 * q : 4 * q + 4, :].bitcast(I32),
            )
        nc.gpsimd.tensor_scalar(
            out=step_rows[0:ROW_TILES, :], in0=step_raw[:], scalar1=-1.0, scalar2=0.0, op0=MULT, op1=ADD
        )
        for i in range(3, 5):
            mom_t.append(load_rows("mom", mom, i))
        r_codes = []
        for c in range(GROUPS):
            t = resident("r_codes%d" % c, [P, GROUPS, BANK], U32)
            src = r_words.rearrange("g p n t -> p g (n t)")[:, :, 4 * BANK * c : 4 * BANK * (c + 1)]
            nc.sync.dma_start(out=t[:].bitcast(I32), in_=src.bitcast(I32))
            r_codes.append(t)
        w_t = []
        for i in range(ROW_TILES):
            w_t.append(load_rows("w", w, i))
            if 5 + i < ROW_TILES:
                mom_t.append(load_rows("mom", mom, 5 + i))

        neg_step = resident("neg_step", [P, ROW_TILES], F32)
        h_rows = {}
        h_codes = {}
        h_scales = {}
        waiting = []

        def new_bank():
            bank = psum.tile([P, BANK], F32, name="bank")
            return bank

        def flush():
            while waiting:
                quantize(*waiting.pop(0))

        def left(i):
            if i < A_FIRST:
                a_t, a0 = a_first, 2 * P * i
            else:
                a_t, a0 = a_rest, 2 * P * (i - A_FIRST)
            for g in range(GROUPS):
                if g == 0:
                    g_t, g0 = g_first, 0
                else:
                    g_t, g0 = g_rest, 2 * BANK * (g - 1)
                bank = new_bank()
                for k in range(LEFT_PASSES):
                    nc.tensor.matmul_mx(
                        out=bank[:],
                        lhsT=a_t[:, k, a0 : a0 + 2 * P].bitcast(FP4X4),
                        lhsT_scale=a_plane[:, k, i * P : (i + 1) * P],
                        rhs=g_t[:, k, g0 : g0 + 2 * BANK].bitcast(FP4X4),
                        rhs_scale=g_plane[:, k, g * BANK : (g + 1) * BANK],
                        start=(k == 0),
                        stop=(k == LEFT_PASSES - 1),
                    )
                h = stage.tile([P, 2, P, 2], BF16, name="h_rows", bufs=15, align_bytes=64)
                mom_v = mom_t[i][:, g * BANK : (g + 1) * BANK].rearrange("q (p u e) -> q u p e", u=2, e=2)
                bank_v = bank[:].rearrange("q (p u e) -> q u p e", u=2, e=2)
                for u in range(2):
                    nc.vector.scalar_tensor_tensor(
                        out=h[:, u], in0=mom_v[:, u], scalar=BETA, in1=bank_v[:, u], op0=MULT, op1=ADD
                    )
                h_rows[i, g] = h
                flush()

        def quantize(pair, g, turned):
            codes = resident("h_codes%d_%d" % (pair, g), [P, 2 * P], U32)
            scales = resident("h_scales%d_%d" % (pair, g), [P, 2 * P], U8)
            nc.vector.quantize_mx(out=codes[:].bitcast(FP8X4), scales=scales[:], in_=turned[:])
            h_codes[pair, g] = codes
            h_scales[pair, g] = scales

        def turn(pair):
            if pair == 0:
                bank = new_bank()
                nc.tensor.transpose(bank[:, 0:P], step_rows[:], ident[:])
                nc.scalar.copy(out=neg_step[:], in_=bank[:, 0:ROW_TILES])
            for g in range(GROUPS):
                bank = new_bank()
                for half in range(2):
                    words = h_rows[2 * pair + half, g][:].rearrange("q u p e -> q (u p e)").bitcast(F32)
                    for u in range(2):
                        c0 = (2 * u + half) * P
                        nc.tensor.transpose(bank[:, c0 : c0 + P], words[:, u * P : (u + 1) * P], ident[:])
                turned = stage.tile([P, 2 * P * 4], BF16, name="turned", bufs=4, align_bytes=64)
                nc.scalar.copy(
                    out=turned[:].bitcast(F32).rearrange("p (i u) -> p i u", u=2),
                    in_=bank[:].rearrange("p (u i) -> p i u", u=2),
                )
                if g < GROUPS - 1:
                    quantize(pair, g, turned)
                else:
                    waiting.append((pair, g, turned))

        def right(i):
            pair, half = divmod(i, 2)
            rows = slice(half * P, (half + 1) * P)
            for c in range(GROUPS):
                cols = slice(c * BANK, (c + 1) * BANK)
                bank = new_bank()
                for g in range(GROUPS):
                    nc.tensor.matmul_mx(
                        out=bank[:],
                        lhsT=h_codes[pair, g][:, rows].bitcast(FP8X4),
                        lhsT_scale=h_scales[pair, g][:, rows],
                        rhs=r_codes[c][:, g, :].bitcast(FP8X4),
                        rhs_scale=r_plane[4 * g : P, cols],
                        start=(g == 0),
                        stop=(g == GROUPS - 1),
                    )
                result = stage.tile([P, BANK], F32, name="result", bufs=12)
                nc.vector.scalar_tensor_tensor(
                    out=result[:], in0=bank[:], scalar=neg_step[:, i : i + 1], in1=w_t[i][:, cols], op0=MULT, op1=ADD
                )
                nc.sync.dma_start(out=out[i * P : (i + 1) * P, cols], in_=result[:])
                flush()

        left(0)
        left(1)
        left(2)
        turn(0)
        left(3)
        left(4)
        turn(1)
        right(0)
        left(5)
        right(1)
        left(6)
        turn(2)
        right(2)
        left(7)
        right(3)
        turn(3)
        for i in range(4, ROW_TILES):
            right(i)
